import numpy as np
import ml_dtypes


def mxq(x, axis, fmt="e4m3"):
    dtype, down = {"e4m3": (ml_dtypes.float8_e4m3fn, 7), "e5m2": (ml_dtypes.float8_e5m2, 14)}[fmt]
    v = np.moveaxis(np.asarray(x, np.float32).astype(ml_dtypes.bfloat16).astype(np.float64), axis, -1)
    blocks = v.reshape(v.shape[:-1] + (-1, 32))
    amax = np.abs(blocks).max(-1, keepdims=True)
    byte = np.maximum(np.where(amax > 0, np.frexp(amax)[1] - 1 + 127, 0) - down, 1)
    scale = np.exp2(byte - 127.0)
    codes = (blocks / scale).astype(np.float32).astype(dtype).astype(np.float64)
    return np.moveaxis((codes * scale).reshape(v.shape), -1, axis)


WIDE = False


def mx_kscale(k):
    if not WIDE:
        return np.ones(k)
    levels = np.array([10, -10, 5, -5, 0])
    if k % 512:
        return np.exp2(np.random.permutation(np.resize(levels, k // 32))).repeat(32)
    a = np.empty((k // 512, 16))
    for p in range(k // 512):
        a[p, :8] = np.random.permutation(np.resize(levels, 8))
        for g in range(8):
            far = levels[np.abs(levels - a[p, g]) >= 10]
            a[p, g + 8] = far[np.random.randint(len(far))]
    return np.exp2(a.ravel()).repeat(32)


def f64(x):
    return np.asarray(x).astype(np.float64)


def striped(idx):
    return np.tile(idx.reshape(-1, 16).T, (8, 1)).astype(np.uint16)


def unstriped(offs):
    return offs[:16].T.reshape(-1).astype(np.int64)


def striped8(idx):
    return np.concatenate([x.reshape(-1, 16).T for x in idx]).astype(np.uint16)


def runs(offs, k):
    lists = np.stack([offs[16 * r : 16 * r + 16].T.reshape(-1) for r in range(8)]).astype(np.int64)
    return lists[np.arange(k) % 512 // 64]


def pack_weight(w):
    k, n = w.shape
    w = f64(np.asarray(w, np.float32).astype(ml_dtypes.bfloat16)).reshape(k // 32, 32, n)
    amax = np.abs(w).max(1)
    byte = np.clip(np.where(amax > 0, np.frexp(amax)[1] - 1 + 127 - 7, 1), 1, 254)
    scaled = (w * np.exp2(127.0 - byte)[:, None, :]).reshape(k, n).astype(np.float32)
    words = np.ascontiguousarray(scaled.reshape(k // 512, 128, 4, n).transpose(0, 1, 3, 2)).astype(ml_dtypes.float8_e4m3fn).view(np.uint8)
    return words, np.ascontiguousarray(byte.astype(np.uint8).reshape(k // 512, 16, n))


def unpack_weight(words, scales):
    g, p, n, _ = words.shape
    vals = np.ascontiguousarray(words).view(ml_dtypes.float8_e4m3fn).astype(np.float64) * np.repeat(np.exp2(scales.astype(np.float64) - 127.0), 8, axis=1)[..., None]
    return vals.transpose(0, 1, 3, 2).reshape(g * 512, n)


def sigmoid(v):
    return 1.0 / (1.0 + np.exp(-np.maximum(v, -700.0)))

def planes(y):
    n, m = y.shape
    v = y.astype(np.float32).astype(ml_dtypes.bfloat16).astype(np.float64).reshape(n // 32, 32, m)
    top = np.abs(v).max(1)
    byte = np.clip(np.where(top > 0, np.frexp(top)[1] - 1 + 127 - 7, 1), 1, 254)
    codes = (v * np.exp2(127.0 - byte)[:, None, :]).reshape(n, m).astype(np.float32).astype(ml_dtypes.float8_e4m3fn).view(np.uint8)
    words = codes.reshape(n // 512, 128, 4, m).transpose(0, 1, 3, 2)
    return np.ascontiguousarray(words), np.ascontiguousarray(byte.astype(np.uint8).reshape(n // 512, 16, m))


K, T, S, N, H = 512, 2048, 512, 512, 512


def setup_inputs():
    n = np.random.standard_normal
    s = mx_kscale(K)[:, None]
    u = mx_kscale(S)
    packed_xT = pack_weight(n((K, T)) * s)
    return {
        "x_words": packed_xT[0],
        "x_scales": packed_xT[1],
        "wa": (n((K, H)) / np.sqrt(K) / s).astype(np.float32),
        "wb": (n((K, N)) / np.sqrt(K) / s).astype(np.float32),
        "gt": (np.random.uniform(0.5, 1.5, (S, 1)) * u[:, None]).astype(np.float32),
        "gi": (np.random.uniform(0.5, 1.5, (S, 1)) / u[:, None]).astype(np.float32),
        "offs": striped(np.random.permutation(T)[:S]),
        "two": striped(np.random.permutation(T)[:S]),
        "n1": striped8(np.stack([np.random.permutation(H) for _ in range(8)])),
        "n2": striped8(np.stack([np.random.permutation(H) for _ in range(8)])),
        "n3": striped8(np.stack([np.random.permutation(H) for _ in range(8)])),
        "n4": striped8(np.stack([np.random.permutation(N) for _ in range(8)])),
        "n5": striped8(np.stack([np.random.permutation(N) for _ in range(8)])),
    }


def reference(x_words, x_scales, wa, wb, gt, gi, offs, two, n1, n2, n3, n4, n5):
    xq = unpack_weight(x_words, x_scales)[:, unstriped(offs)]
    a = xq.T @ mxq(f64(wa), 0, "e4m3")
    pa = a[np.arange(S)[:, None], runs(n1, S)]
    z = f64(gt) * (pa + (sigmoid(a[np.arange(S)[:, None], runs(n2, S)])) * (a[np.arange(S)[:, None], runs(n3, S)] - pa))
    x_two = unpack_weight(x_words, x_scales)[:, unstriped(two)]
    b = x_two.T @ mxq(f64(wb), 0, "e4m3")
    z2 = f64(gi) * b
    cv = 0.0625 * ((mxq(z, 0, "e4m3").T @ mxq(z2, 0, "e4m3")))
    out_0 = np.maximum(cv * (sigmoid(cv[np.arange(H)[:, None], runs(n4, H)])), cv[np.arange(H)[:, None], runs(n5, H)])
    return (out_0,) + planes(out_0)

@@ -1,0 +1,198 @@
+from contextlib import ExitStack
+
+import concourse.mybir as mybir
+
+F32 = mybir.dt.float32
+BF16 = mybir.dt.bfloat16
+I32 = mybir.dt.int32
+U32 = mybir.dt.uint32
+U16 = mybir.dt.uint16
+U8 = mybir.dt.uint8
+FP8X4 = mybir.dt.float8_e4m3fn_x4
+ALU = mybir.AluOpType
+ACT = mybir.ActivationFunctionType
+
+P = 128
+PACK = 4
+T = 2048
+W = 512
+HALF = W // 2
+LIST_COLS = W // 16
+FLOPS = 3 * 2 * 512 * 512 * 512
+
+
+def tile_picked_momlerpgmax_none_po_kernel(
+    tc, x_words, x_scales, wa, wb, gt, gi, offs, two, n1, n2, n3, n4, n5, out_0, out_1, out_2
+):
+    nc = tc.nc
+    with ExitStack() as ctx:
+        keep = ctx.enter_context(tc.tile_pool(name="keep", bufs=1))
+        psum = ctx.enter_context(tc.psum_pool(name="psum", bufs=1))
+
+        def load_list(name, src):
+            tile = keep.tile([P, LIST_COLS], U16, name=name)
+            nc.sync.dma_start(tile[:], src)
+            return tile
+
+        def cols(h):
+            return slice(h * HALF, (h + 1) * HALF)
+
+        def entries(tile, h):
+            return tile[:, h * (LIST_COLS // 2) : (h + 1) * (LIST_COLS // 2)]
+
+        xs = keep.tile([P, T], U8, name="xs", align_bytes=64)
+        nc.vector.memset(xs[:].bitcast(I32), 0)
+        warm_in = keep.tile([P, 1], F32, name="warm_in")
+        warm_out = keep.tile([P, 1], F32, name="warm_out")
+        nc.vector.memset(warm_in[:], 0.0)
+        for q in range(4):
+            nc.scalar.dma_start(xs[32 * q : 32 * q + 4, :].bitcast(I32), x_scales[0, 4 * q : 4 * q + 4, :].bitcast(I32))
+        nc.scalar.activation(warm_out[:], warm_in[:], ACT.Sigmoid)
+
+        l_offs = load_list("l_offs", offs)
+        l_two = load_list("l_two", two)
+        l_n1 = load_list("l_n1", n1)
+        l_n3 = load_list("l_n3", n3)
+
+        def load_weight(name, w, h):
+            raw = keep.tile([P, PACK, HALF], F32, name=f"{name}_raw{h}")
+            nc.sync.dma_start(raw[:], w.rearrange("(p j) n -> p j n", j=PACK)[:, :, cols(h)])
+            return raw
+
+        wa_raw = [load_weight("wa", wa, h) for h in range(2)]
+        xw = keep.tile([P, T], I32, name="xw", align_bytes=64)
+        nc.sync.dma_start(xw[:], x_words[0].rearrange("p n r -> p (n r)").bitcast(I32))
+        l_n2 = load_list("l_n2", n2)
+        gt_sb = keep.tile([P, PACK], F32, name="gt_sb")
+        nc.sync.dma_start(gt_sb[:], gt.rearrange("(p t) o -> p (t o)", t=PACK))
+        wb_raw = [load_weight("wb", wb, h) for h in range(2)]
+        gi_sb = keep.tile([P, PACK], F32, name="gi_sb")
+        nc.sync.dma_start(gi_sb[:], gi.rearrange("(p t) o -> p (t o)", t=PACK))
+        l_n4 = load_list("l_n4", n4)
+        l_n5 = load_list("l_n5", n5)
+
+        picked_bytes = keep.tile([P, 2, W], U8, name="picked_bytes", align_bytes=64)
+        dealt_bytes = keep.tile([P, 2, PACK, P], U8, name="dealt_bytes", align_bytes=64)
+        for l, lst in enumerate((l_offs, l_two)):
+            nc.vector.tensor_copy(picked_bytes[:, l, :], xs[:].indirect(lst[:]))
+        nc.vector.tensor_copy(dealt_bytes[:], picked_bytes[:].rearrange("p l (m t) -> p l t m", t=PACK))
+
+        def pick_words(name, lst):
+            words = keep.tile([P, PACK, P], U32, name=name, align_bytes=64)
+            nc.vector.tensor_copy(words[:].rearrange("p t m -> p m t"), xw[:].bitcast(U32).indirect(lst[:]))
+            return words
+
+        def interleave(eng, dst, src):
+            d = dst.rearrange("p (c i) t -> p c t i", i=4)
+            s = src.rearrange("p t (c i) -> p c t i", i=4)
+            if eng is nc.scalar:
+                nc.scalar.copy(d, s)
+            else:
+                nc.vector.tensor_copy(d, s)
+
+        def quantize(codes, scales, grouped):
+            nc.vector.quantize_mx(out=codes.bitcast(FP8X4), scales=scales, in_=grouped.rearrange("p n t -> p (n t)"))
+
+        def quantize_weight(name, raw):
+            codes = keep.tile([P, W], U32, name=f"{name}_codes", align_bytes=64)
+            scales = keep.tile([P, W], U8, name=f"{name}_scales", align_bytes=64)
+            for h in range(2):
+                grouped = keep.tile([P, HALF, PACK], BF16, name=f"{name}_grouped{h}", align_bytes=64)
+                interleave(nc.scalar, grouped[:], raw[h][:])
+                quantize(codes[:, cols(h)], scales[:, cols(h)], grouped[:])
+            return codes, scales
+
+        def product(bank, lhs_codes, lhs_scales, rhs_codes, rhs_scales):
+            nc.tensor.matmul_mx(
+                out=bank, lhsT=lhs_codes.bitcast(FP8X4), lhsT_scale=lhs_scales,
+                rhs=rhs_codes.bitcast(FP8X4), rhs_scale=rhs_scales, start=True, stop=True,
+            )
+
+        xa = pick_words("xa", l_offs)
+        wa_codes, wa_scales = quantize_weight("wa", wa_raw)
+        a_banks = []
+        for t in range(PACK):
+            bank = psum.tile([P, W], F32, name=f"a_bank{t}", tag=f"bank{t}")
+            product(bank[:], xa[:, t, :], dealt_bytes[:, 0, t, :], wa_codes[:], wa_scales[:])
+            a_banks.append(bank)
+        xb = pick_words("xb", l_two)
+
+        pa = keep.tile([P, PACK, W], F32, name="pa")
+        diff = keep.tile([P, PACK, W], F32, name="diff")
+        gate = keep.tile([P, PACK, W], F32, name="gate")
+        step = keep.tile([P, PACK, W], F32, name="step")
+
+        def look_up_a(t):
+            ga = keep.tile([P, W], F32, name=f"ga{t}")
+            a = keep.tile([P, W], F32, name=f"a{t}")
+            nc.scalar.activation(ga[:], a_banks[t][:], ACT.Copy, scale=gt_sb[:, t : t + 1])
+            nc.scalar.copy(a[:], a_banks[t][:])
+            for h in range(2):
+                nc.scalar.activation(gate[:, t, cols(h)], a[:].indirect(entries(l_n2, h)), ACT.Sigmoid)
+            for h in range(2):
+                nc.vector.tensor_copy(pa[:, t, cols(h)], ga[:].indirect(entries(l_n1, h)))
+            for h in range(2):
+                nc.vector.tensor_tensor(diff[:, t, cols(h)], ga[:].indirect(entries(l_n3, h)), pa[:, t, cols(h)], ALU.subtract)
+            nc.vector.tensor_tensor(step[:, t, :], diff[:, t, :], gate[:, t, :], ALU.mult)
+
+        look_up_a(0)
+        look_up_a(1)
+        wb_codes, wb_scales = quantize_weight("wb", wb_raw)
+        z2_rows = keep.tile([P, PACK, W], BF16, name="z2_rows")
+        b_banks = []
+        for t in range(PACK):
+            bank = psum.tile([P, W], F32, name=f"b_bank{t}")
+            product(bank[:], xb[:, t, :], dealt_bytes[:, 1, t, :], wb_codes[:], wb_scales[:])
+            b_banks.append(bank)
+        look_up_a(2)
+        look_up_a(3)
+        for t in range(PACK):
+            nc.scalar.activation(z2_rows[:, t, :], b_banks[t][:], ACT.Copy, scale=gi_sb[:, t : t + 1])
+        z2_grouped = keep.tile([P, W, PACK], BF16, name="z2_grouped", align_bytes=64)
+        interleave(nc.scalar, z2_grouped[:], z2_rows[:])
+
+        z_grouped = keep.tile([P, PACK, P, PACK], BF16, name="z_grouped", align_bytes=64)
+        nc.vector.tensor_tensor(
+            z_grouped[:].rearrange("p i m t -> p m t i"),
+            pa[:].rearrange("p t (m i) -> p m t i", i=PACK),
+            step[:].rearrange("p t (m i) -> p m t i", i=PACK),
+            ALU.add,
+        )
+        z2_codes = keep.tile([P, W], U32, name="z2_codes", align_bytes=64)
+        z2_scales = keep.tile([P, W], U8, name="z2_scales", align_bytes=64)
+        quantize(z2_codes[:], z2_scales[:], z2_grouped[:])
+        cv_banks = []
+        for i in range(PACK):
+            z_codes = keep.tile([P, P], U32, name=f"z_codes{i}", align_bytes=64)
+            z_scales = keep.tile([P, P], U8, name=f"z_scales{i}", align_bytes=64)
+            quantize(z_codes[:], z_scales[:], z_grouped[:, i, :, :])
+            bank = psum.tile([P, W], F32, name=f"cv_bank{i}", tag=f"bank{i}")
+            product(bank[:], z_codes[:], z_scales[:], z2_codes[:], z2_scales[:])
+            cv_banks.append(bank)
+
+        cv = [keep.tile([P, W], F32, name=f"cv{i}") for i in range(PACK)]
+        out_codes = keep.tile([P, W], U32, name="out_codes", align_bytes=64)
+        out_scales = keep.tile([P, W], U8, name="out_scales", align_bytes=64)
+        out_rows = out_0.rearrange("(p i) n -> p i n", i=PACK)
+        out_words = out_1[0].rearrange("p n r -> p (n r)").bitcast(I32)
+        for h in range(2):
+            gate2 = keep.tile([P, PACK, HALF], F32, name=f"gate2_{h}")
+            other = keep.tile([P, PACK, HALF], F32, name=f"other{h}")
+            gated = keep.tile([P, PACK, HALF], F32, name=f"gated{h}")
+            result = keep.tile([P, PACK, HALF], F32, name=f"result{h}")
+            for i in range(PACK):
+                if h == 0:
+                    nc.scalar.activation(cv[i][:], cv_banks[i][:], ACT.Copy, scale=0.0625)
+                nc.scalar.activation(gate2[:, i, :], cv[i][:].indirect(entries(l_n4, h)), ACT.Sigmoid)
+                nc.vector.tensor_copy(other[:, i, :], cv[i][:].indirect(entries(l_n5, h)))
+                nc.vector.tensor_tensor(gated[:, i, :], cv[i][:, cols(h)], gate2[:, i, :], ALU.mult)
+                if i % 2 == 1:
+                    nc.vector.tensor_tensor(result[:, i - 1 : i + 1, :], gated[:, i - 1 : i + 1, :], other[:, i - 1 : i + 1, :], ALU.max)
+            nc.sync.dma_start(out_rows[:, :, cols(h)], result[:])
+            grouped = keep.tile([P, HALF, PACK], BF16, name=f"out_grouped{h}", align_bytes=64)
+            interleave(nc.scalar if h == 0 else nc.vector, grouped[:], result[:])
+            quantize(out_codes[:, cols(h)], out_scales[:, cols(h)], grouped[:])
+            nc.sync.dma_start(out_words[:, cols(h)], out_codes[:, cols(h)].bitcast(I32))
+        for q in range(4):
+            eng = nc.scalar if q % 2 == 0 else nc.sync
+            eng.dma_start(out_2[0, 4 * q : 4 * q + 4, :].bitcast(I32), out_scales[32 * q : 32 * q + 4, :].bitcast(I32))

@@ -62,12 +62,17 @@ def tile_picked_momlerpgmax_none_po_kernel(
         wa_raw = [load_weight("wa", wa, h) for h in range(2)]
         xw = keep.tile([P, T], I32, name="xw", align_bytes=64)
         nc.sync.dma_start(xw[:], x_words[0].rearrange("p n r -> p (n r)").bitcast(I32))
-        l_n2 = load_list("l_n2", n2)
-        gt_sb = keep.tile([P, PACK], F32, name="gt_sb")
-        nc.sync.dma_start(gt_sb[:], gt.rearrange("(p t) o -> p (t o)", t=PACK))
+
+        def load_place_weights(name, g, t):
+            tile = keep.tile([P, 1], F32, name=f"{name}{t}")
+            nc.sync.dma_start(tile[:], g.rearrange("(b t e) o -> t b e o", t=PACK, e=8)[t])
+            return tile
+
+        gt_sb = [load_place_weights("gt", gt, 0)]
         wb_raw = [load_weight("wb", wb, h) for h in range(2)]
-        gi_sb = keep.tile([P, PACK], F32, name="gi_sb")
-        nc.sync.dma_start(gi_sb[:], gi.rearrange("(p t) o -> p (t o)", t=PACK))
+        l_n2 = load_list("l_n2", n2)
+        gt_sb.extend(load_place_weights("gt", gt, t) for t in range(1, PACK))
+        gi_sb = [load_place_weights("gi", gi, t) for t in range(PACK)]
         l_n4 = load_list("l_n4", n4)
         l_n5 = load_list("l_n5", n5)
 
@@ -75,11 +80,14 @@ def tile_picked_momlerpgmax_none_po_kernel(
         dealt_bytes = keep.tile([P, 2, PACK, P], U8, name="dealt_bytes", align_bytes=64)
         for l, lst in enumerate((l_offs, l_two)):
             nc.vector.tensor_copy(picked_bytes[:, l, :], xs[:].indirect(lst[:]))
-        nc.vector.tensor_copy(dealt_bytes[:], picked_bytes[:].rearrange("p l (m t) -> p l t m", t=PACK))
+        nc.vector.tensor_copy(
+            dealt_bytes[:].bitcast(I32).rearrange("p l t (b e) -> p l t b e", e=2),
+            picked_bytes[:].bitcast(I32).rearrange("p l (b t e) -> p l t b e", t=PACK, e=2),
+        )
 
         def pick_words(name, lst):
             words = keep.tile([P, PACK, P], U32, name=name, align_bytes=64)
-            nc.vector.tensor_copy(words[:].rearrange("p t m -> p m t"), xw[:].bitcast(U32).indirect(lst[:]))
+            nc.vector.tensor_copy(words[:].rearrange("p t (b e) -> p b t e", e=8), xw[:].bitcast(U32).indirect(lst[:]))
             return words
 
         def interleave(eng, dst, src):
@@ -93,14 +101,15 @@ def tile_picked_momlerpgmax_none_po_kernel(
         def quantize(codes, scales, grouped):
             nc.vector.quantize_mx(out=codes.bitcast(FP8X4), scales=scales, in_=grouped.rearrange("p n t -> p (n t)"))
 
-        def quantize_weight(name, raw):
-            codes = keep.tile([P, W], U32, name=f"{name}_codes", align_bytes=64)
-            scales = keep.tile([P, W], U8, name=f"{name}_scales", align_bytes=64)
-            for h in range(2):
-                grouped = keep.tile([P, HALF, PACK], BF16, name=f"{name}_grouped{h}", align_bytes=64)
-                interleave(nc.scalar, grouped[:], raw[h][:])
-                quantize(codes[:, cols(h)], scales[:, cols(h)], grouped[:])
+        def operand(name, width):
+            codes = keep.tile([P, width], U32, name=f"{name}_codes", align_bytes=64)
+            scales = keep.tile([P, width], U8, name=f"{name}_scales", align_bytes=64)
             return codes, scales
+
+        def regroup_weight(name, raw):
+            grouped = keep.tile([P, HALF, PACK], BF16, name=name, align_bytes=64)
+            interleave(nc.scalar, grouped[:], raw[:])
+            return grouped
 
         def product(bank, lhs_codes, lhs_scales, rhs_codes, rhs_scales):
             nc.tensor.matmul_mx(
@@ -109,7 +118,9 @@ def tile_picked_momlerpgmax_none_po_kernel(
             )
 
         xa = pick_words("xa", l_offs)
-        wa_codes, wa_scales = quantize_weight("wa", wa_raw)
+        wa_codes, wa_scales = operand("wa", W)
+        for h in range(2):
+            quantize(wa_codes[:, cols(h)], wa_scales[:, cols(h)], regroup_weight(f"wa_grouped{h}", wa_raw[h])[:])
         a_banks = []
         for t in range(PACK):
             bank = psum.tile([P, W], F32, name=f"a_bank{t}", tag=f"bank{t}")
@@ -125,7 +136,7 @@ def tile_picked_momlerpgmax_none_po_kernel(
         def look_up_a(t):
             ga = keep.tile([P, W], F32, name=f"ga{t}")
             a = keep.tile([P, W], F32, name=f"a{t}")
-            nc.scalar.activation(ga[:], a_banks[t][:], ACT.Copy, scale=gt_sb[:, t : t + 1])
+            nc.scalar.activation(ga[:], a_banks[t][:], ACT.Copy, scale=gt_sb[t][:])
             nc.scalar.copy(a[:], a_banks[t][:])
             for h in range(2):
                 nc.scalar.activation(gate[:, t, cols(h)], a[:].indirect(entries(l_n2, h)), ACT.Sigmoid)
@@ -133,11 +144,15 @@ def tile_picked_momlerpgmax_none_po_kernel(
                 nc.vector.tensor_copy(pa[:, t, cols(h)], ga[:].indirect(entries(l_n1, h)))
             for h in range(2):
                 nc.vector.tensor_tensor(diff[:, t, cols(h)], ga[:].indirect(entries(l_n3, h)), pa[:, t, cols(h)], ALU.subtract)
-            nc.vector.tensor_tensor(step[:, t, :], diff[:, t, :], gate[:, t, :], ALU.mult)
+            for h in range(2):
+                nc.vector.tensor_tensor(step[:, t, cols(h)], diff[:, t, cols(h)], gate[:, t, cols(h)], ALU.mult)
 
+        wb_codes, wb_scales = operand("wb", W)
+        quantize(wb_codes[:, cols(0)], wb_scales[:, cols(0)], regroup_weight("wb_grouped0", wb_raw[0])[:])
         look_up_a(0)
+        wb_grouped1 = regroup_weight("wb_grouped1", wb_raw[1])
         look_up_a(1)
-        wb_codes, wb_scales = quantize_weight("wb", wb_raw)
+        quantize(wb_codes[:, cols(1)], wb_scales[:, cols(1)], wb_grouped1[:])
         z2_rows = keep.tile([P, PACK, W], BF16, name="z2_rows")
         b_banks = []
         for t in range(PACK):
@@ -147,17 +162,18 @@ def tile_picked_momlerpgmax_none_po_kernel(
         look_up_a(2)
         look_up_a(3)
         for t in range(PACK):
-            nc.scalar.activation(z2_rows[:, t, :], b_banks[t][:], ACT.Copy, scale=gi_sb[:, t : t + 1])
+            nc.scalar.activation(z2_rows[:, t, :], b_banks[t][:], ACT.Copy, scale=gi_sb[t][:])
         z2_grouped = keep.tile([P, W, PACK], BF16, name="z2_grouped", align_bytes=64)
         interleave(nc.scalar, z2_grouped[:], z2_rows[:])
 
         z_grouped = keep.tile([P, PACK, P, PACK], BF16, name="z_grouped", align_bytes=64)
-        nc.vector.tensor_tensor(
-            z_grouped[:].rearrange("p i m t -> p m t i"),
-            pa[:].rearrange("p t (m i) -> p m t i", i=PACK),
-            step[:].rearrange("p t (m i) -> p m t i", i=PACK),
-            ALU.add,
-        )
+        for h in range(2):
+            nc.vector.tensor_tensor(
+                z_grouped[:, :, h * (P // 2) : (h + 1) * (P // 2), :].rearrange("p i m t -> p m t i"),
+                pa[:, :, cols(h)].rearrange("p t (m i) -> p m t i", i=PACK),
+                step[:, :, cols(h)].rearrange("p t (m i) -> p m t i", i=PACK),
+                ALU.add,
+            )
         z2_codes = keep.tile([P, W], U32, name="z2_codes", align_bytes=64)
         z2_scales = keep.tile([P, W], U8, name="z2_scales", align_bytes=64)
         quantize(z2_codes[:], z2_scales[:], z2_grouped[:])
@@ -175,24 +191,44 @@ def tile_picked_momlerpgmax_none_po_kernel(
         out_scales = keep.tile([P, W], U8, name="out_scales", align_bytes=64)
         out_rows = out_0.rearrange("(p i) n -> p i n", i=PACK)
         out_words = out_1[0].rearrange("p n r -> p (n r)").bitcast(I32)
+        nc.vector.tensor_scalar(cv[0][:], cv_banks[0][:], 0.0625, None, ALU.mult)
+        results = [keep.tile([P, PACK, HALF], F32, name=f"result{h}") for h in range(2)]
+
+        def hand_on(name, eng, h, first, width):
+            grouped = keep.tile([P, width, PACK], BF16, name=name, align_bytes=64)
+            interleave(eng, grouped[:], results[h][:, :, first : first + width])
+            c = slice(h * HALF + first, h * HALF + first + width)
+            quantize(out_codes[:, c], out_scales[:, c], grouped[:])
+
+        def store_words(h):
+            nc.sync.dma_start(out_words[:, cols(h)], out_codes[:, cols(h)].bitcast(I32))
+
         for h in range(2):
             gate2 = keep.tile([P, PACK, HALF], F32, name=f"gate2_{h}")
             other = keep.tile([P, PACK, HALF], F32, name=f"other{h}")
             gated = keep.tile([P, PACK, HALF], F32, name=f"gated{h}")
-            result = keep.tile([P, PACK, HALF], F32, name=f"result{h}")
-            for i in range(PACK):
-                if h == 0:
-                    nc.scalar.activation(cv[i][:], cv_banks[i][:], ACT.Copy, scale=0.0625)
-                nc.scalar.activation(gate2[:, i, :], cv[i][:].indirect(entries(l_n4, h)), ACT.Sigmoid)
-                nc.vector.tensor_copy(other[:, i, :], cv[i][:].indirect(entries(l_n5, h)))
-                nc.vector.tensor_tensor(gated[:, i, :], cv[i][:, cols(h)], gate2[:, i, :], ALU.mult)
+            result = results[h]
+
+            def larger(i):
+                nc.vector.tensor_tensor(result[:, i, :], gated[:, i, :], other[:, i, :], ALU.max)
                 if i % 2 == 1:
-                    nc.vector.tensor_tensor(result[:, i - 1 : i + 1, :], gated[:, i - 1 : i + 1, :], other[:, i - 1 : i + 1, :], ALU.max)
-            nc.sync.dma_start(out_rows[:, :, cols(h)], result[:])
-            grouped = keep.tile([P, HALF, PACK], BF16, name=f"out_grouped{h}", align_bytes=64)
-            interleave(nc.scalar if h == 0 else nc.vector, grouped[:], result[:])
-            quantize(out_codes[:, cols(h)], out_scales[:, cols(h)], grouped[:])
-            nc.sync.dma_start(out_words[:, cols(h)], out_codes[:, cols(h)].bitcast(I32))
+                    nc.sync.dma_start(out_rows[:, i - 1 : i + 1, cols(h)], result[:, i - 1 : i + 1, :])
+
+            for i in range(PACK):
+                if h == 0 and i + 1 < PACK:
+                    nc.scalar.activation(cv[i + 1][:], cv_banks[i + 1][:], ACT.Copy, scale=0.0625)
+                nc.scalar.activation(gate2[:, i, :], cv[i][:].indirect(entries(l_n4, h)), ACT.Sigmoid)
+                nc.vector.tensor_tensor(gated[:, i, :], cv[i][:, cols(h)], gate2[:, i, :], ALU.mult)
+                nc.vector.tensor_copy(other[:, i, :], cv[i][:].indirect(entries(l_n5, h)))
+                if i > 0:
+                    larger(i - 1)
+            if h == 1:
+                hand_on("out_grouped0", nc.scalar, 0, 0, HALF)
+                store_words(0)
+            larger(PACK - 1)
+        hand_on("out_grouped1", nc.vector, 1, 0, P)
+        hand_on("out_grouped2", nc.scalar, 1, P, P)
+        store_words(1)
         for q in range(4):
             eng = nc.scalar if q % 2 == 0 else nc.sync
             eng.dma_start(out_2[0, 4 * q : 4 * q + 4, :].bitcast(I32), out_scales[32 * q : 32 * q + 4, :].bitcast(I32))

from contextlib import ExitStack

import concourse.mybir as mybir

F32 = mybir.dt.float32
BF16 = mybir.dt.bfloat16
I32 = mybir.dt.int32
U32 = mybir.dt.uint32
U16 = mybir.dt.uint16
U8 = mybir.dt.uint8
FP8X4 = mybir.dt.float8_e4m3fn_x4
ALU = mybir.AluOpType
ACT = mybir.ActivationFunctionType

P = 128
PACK = 4
T = 2048
W = 512
HALF = W // 2
LIST_COLS = W // 16
FLOPS = 3 * 2 * 512 * 512 * 512


def tile_picked_momlerpgmax_none_po_kernel(
    tc, x_words, x_scales, wa, wb, gt, gi, offs, two, n1, n2, n3, n4, n5, out_0, out_1, out_2
):
    nc = tc.nc
    with ExitStack() as ctx:
        keep = ctx.enter_context(tc.tile_pool(name="keep", bufs=1))
        psum = ctx.enter_context(tc.psum_pool(name="psum", bufs=1))

        def load_list(name, src):
            tile = keep.tile([P, LIST_COLS], U16, name=name)
            nc.sync.dma_start(tile[:], src)
            return tile

        def cols(h):
            return slice(h * HALF, (h + 1) * HALF)

        def entries(tile, h):
            return tile[:, h * (LIST_COLS // 2) : (h + 1) * (LIST_COLS // 2)]

        xs = keep.tile([P, T], U8, name="xs", align_bytes=64)
        nc.vector.memset(xs[:].bitcast(I32), 0)
        warm_in = keep.tile([P, 1], F32, name="warm_in")
        warm_out = keep.tile([P, 1], F32, name="warm_out")
        nc.vector.memset(warm_in[:], 0.0)
        for q in range(4):
            nc.scalar.dma_start(xs[32 * q : 32 * q + 4, :].bitcast(I32), x_scales[0, 4 * q : 4 * q + 4, :].bitcast(I32))
        nc.scalar.activation(warm_out[:], warm_in[:], ACT.Sigmoid)

        l_offs = load_list("l_offs", offs)
        l_two = load_list("l_two", two)
        l_n1 = load_list("l_n1", n1)
        l_n3 = load_list("l_n3", n3)

        def load_weight(name, w, h):
            raw = keep.tile([P, PACK, HALF], F32, name=f"{name}_raw{h}")
            nc.sync.dma_start(raw[:], w.rearrange("(p j) n -> p j n", j=PACK)[:, :, cols(h)])
            return raw

        wa_raw = [load_weight("wa", wa, h) for h in range(2)]
        xw = keep.tile([P, T], I32, name="xw", align_bytes=64)
        nc.sync.dma_start(xw[:], x_words[0].rearrange("p n r -> p (n r)").bitcast(I32))

        def load_place_weights(name, g, t):
            tile = keep.tile([P, 1], F32, name=f"{name}{t}")
            nc.sync.dma_start(tile[:], g.rearrange("(b t e) o -> t b e o", t=PACK, e=8)[t])
            return tile

        gt_sb = [load_place_weights("gt", gt, 0)]
        wb_raw = [load_weight("wb", wb, h) for h in range(2)]
        l_n2 = load_list("l_n2", n2)
        gt_sb.extend(load_place_weights("gt", gt, t) for t in range(1, PACK))
        gi_sb = [load_place_weights("gi", gi, t) for t in range(PACK)]
        l_n4 = load_list("l_n4", n4)
        l_n5 = load_list("l_n5", n5)

        picked_bytes = keep.tile([P, 2, W], U8, name="picked_bytes", align_bytes=64)
        dealt_bytes = keep.tile([P, 2, PACK, P], U8, name="dealt_bytes", align_bytes=64)
        for l, lst in enumerate((l_offs, l_two)):
            nc.vector.tensor_copy(picked_bytes[:, l, :], xs[:].indirect(lst[:]))
        nc.vector.tensor_copy(
            dealt_bytes[:].bitcast(I32).rearrange("p l t (b e) -> p l t b e", e=2),
            picked_bytes[:].bitcast(I32).rearrange("p l (b t e) -> p l t b e", t=PACK, e=2),
        )

        def pick_words(name, lst):
            words = keep.tile([P, PACK, P], U32, name=name, align_bytes=64)
            nc.vector.tensor_copy(words[:].rearrange("p t (b e) -> p b t e", e=8), xw[:].bitcast(U32).indirect(lst[:]))
            return words

        def interleave(eng, dst, src):
            d = dst.rearrange("p (c i) t -> p c t i", i=4)
            s = src.rearrange("p t (c i) -> p c t i", i=4)
            if eng is nc.scalar:
                nc.scalar.copy(d, s)
            else:
                nc.vector.tensor_copy(d, s)

        def quantize(codes, scales, grouped):
            nc.vector.quantize_mx(out=codes.bitcast(FP8X4), scales=scales, in_=grouped.rearrange("p n t -> p (n t)"))

        def operand(name, width):
            codes = keep.tile([P, width], U32, name=f"{name}_codes", align_bytes=64)
            scales = keep.tile([P, width], U8, name=f"{name}_scales", align_bytes=64)
            return codes, scales

        def regroup_weight(name, raw):
            grouped = keep.tile([P, HALF, PACK], BF16, name=name, align_bytes=64)
            interleave(nc.scalar, grouped[:], raw[:])
            return grouped

        def product(bank, lhs_codes, lhs_scales, rhs_codes, rhs_scales):
            nc.tensor.matmul_mx(
                out=bank, lhsT=lhs_codes.bitcast(FP8X4), lhsT_scale=lhs_scales,
                rhs=rhs_codes.bitcast(FP8X4), rhs_scale=rhs_scales, start=True, stop=True,
            )

        xa = pick_words("xa", l_offs)
        wa_codes, wa_scales = operand("wa", W)
        for h in range(2):
            quantize(wa_codes[:, cols(h)], wa_scales[:, cols(h)], regroup_weight(f"wa_grouped{h}", wa_raw[h])[:])
        a_banks = []
        for t in range(PACK):
            bank = psum.tile([P, W], F32, name=f"a_bank{t}", tag=f"bank{t}")
            product(bank[:], xa[:, t, :], dealt_bytes[:, 0, t, :], wa_codes[:], wa_scales[:])
            a_banks.append(bank)
        xb = pick_words("xb", l_two)

        pa = keep.tile([P, PACK, W], F32, name="pa")
        diff = keep.tile([P, PACK, W], F32, name="diff")
        gate = keep.tile([P, PACK, W], F32, name="gate")
        step = keep.tile([P, PACK, W], F32, name="step")

        def look_up_a(t):
            ga = keep.tile([P, W], F32, name=f"ga{t}")
            a = keep.tile([P, W], F32, name=f"a{t}")
            nc.scalar.activation(ga[:], a_banks[t][:], ACT.Copy, scale=gt_sb[t][:])
            nc.scalar.copy(a[:], a_banks[t][:])
            for h in range(2):
                nc.scalar.activation(gate[:, t, cols(h)], a[:].indirect(entries(l_n2, h)), ACT.Sigmoid)
            for h in range(2):
                nc.vector.tensor_copy(pa[:, t, cols(h)], ga[:].indirect(entries(l_n1, h)))
            for h in range(2):
                nc.vector.tensor_tensor(diff[:, t, cols(h)], ga[:].indirect(entries(l_n3, h)), pa[:, t, cols(h)], ALU.subtract)
            for h in range(2):
                nc.vector.tensor_tensor(step[:, t, cols(h)], diff[:, t, cols(h)], gate[:, t, cols(h)], ALU.mult)

        wb_codes, wb_scales = operand("wb", W)
        quantize(wb_codes[:, cols(0)], wb_scales[:, cols(0)], regroup_weight("wb_grouped0", wb_raw[0])[:])
        look_up_a(0)
        wb_grouped1 = regroup_weight("wb_grouped1", wb_raw[1])
        look_up_a(1)
        quantize(wb_codes[:, cols(1)], wb_scales[:, cols(1)], wb_grouped1[:])
        z2_rows = keep.tile([P, PACK, W], BF16, name="z2_rows")
        b_banks = []
        for t in range(PACK):
            bank = psum.tile([P, W], F32, name=f"b_bank{t}")
            product(bank[:], xb[:, t, :], dealt_bytes[:, 1, t, :], wb_codes[:], wb_scales[:])
            b_banks.append(bank)
        look_up_a(2)
        look_up_a(3)
        for t in range(PACK):
            nc.scalar.activation(z2_rows[:, t, :], b_banks[t][:], ACT.Copy, scale=gi_sb[t][:])
        z2_grouped = keep.tile([P, W, PACK], BF16, name="z2_grouped", align_bytes=64)
        interleave(nc.scalar, z2_grouped[:], z2_rows[:])

        z_grouped = keep.tile([P, PACK, P, PACK], BF16, name="z_grouped", align_bytes=64)
        for h in range(2):
            nc.vector.tensor_tensor(
                z_grouped[:, :, h * (P // 2) : (h + 1) * (P // 2), :].rearrange("p i m t -> p m t i"),
                pa[:, :, cols(h)].rearrange("p t (m i) -> p m t i", i=PACK),
                step[:, :, cols(h)].rearrange("p t (m i) -> p m t i", i=PACK),
                ALU.add,
            )
        z2_codes = keep.tile([P, W], U32, name="z2_codes", align_bytes=64)
        z2_scales = keep.tile([P, W], U8, name="z2_scales", align_bytes=64)
        quantize(z2_codes[:], z2_scales[:], z2_grouped[:])
        cv_banks = []
        for i in range(PACK):
            z_codes = keep.tile([P, P], U32, name=f"z_codes{i}", align_bytes=64)
            z_scales = keep.tile([P, P], U8, name=f"z_scales{i}", align_bytes=64)
            quantize(z_codes[:], z_scales[:], z_grouped[:, i, :, :])
            bank = psum.tile([P, W], F32, name=f"cv_bank{i}", tag=f"bank{i}")
            product(bank[:], z_codes[:], z_scales[:], z2_codes[:], z2_scales[:])
            cv_banks.append(bank)

        cv = [keep.tile([P, W], F32, name=f"cv{i}") for i in range(PACK)]
        out_codes = keep.tile([P, W], U32, name="out_codes", align_bytes=64)
        out_scales = keep.tile([P, W], U8, name="out_scales", align_bytes=64)
        out_rows = out_0.rearrange("(p i) n -> p i n", i=PACK)
        out_words = out_1[0].rearrange("p n r -> p (n r)").bitcast(I32)
        nc.vector.tensor_scalar(cv[0][:], cv_banks[0][:], 0.0625, None, ALU.mult)
        results = [keep.tile([P, PACK, HALF], F32, name=f"result{h}") for h in range(2)]

        def hand_on(name, eng, h, first, width):
            grouped = keep.tile([P, width, PACK], BF16, name=name, align_bytes=64)
            interleave(eng, grouped[:], results[h][:, :, first : first + width])
            c = slice(h * HALF + first, h * HALF + first + width)
            quantize(out_codes[:, c], out_scales[:, c], grouped[:])

        def store_words(h):
            nc.sync.dma_start(out_words[:, cols(h)], out_codes[:, cols(h)].bitcast(I32))

        for h in range(2):
            gate2 = keep.tile([P, PACK, HALF], F32, name=f"gate2_{h}")
            other = keep.tile([P, PACK, HALF], F32, name=f"other{h}")
            gated = keep.tile([P, PACK, HALF], F32, name=f"gated{h}")
            result = results[h]

            def larger(i):
                nc.vector.tensor_tensor(result[:, i, :], gated[:, i, :], other[:, i, :], ALU.max)
                if i % 2 == 1:
                    nc.sync.dma_start(out_rows[:, i - 1 : i + 1, cols(h)], result[:, i - 1 : i + 1, :])

            for i in range(PACK):
                if h == 0 and i + 1 < PACK:
                    nc.scalar.activation(cv[i + 1][:], cv_banks[i + 1][:], ACT.Copy, scale=0.0625)
                nc.scalar.activation(gate2[:, i, :], cv[i][:].indirect(entries(l_n4, h)), ACT.Sigmoid)
                nc.vector.tensor_tensor(gated[:, i, :], cv[i][:, cols(h)], gate2[:, i, :], ALU.mult)
                nc.vector.tensor_copy(other[:, i, :], cv[i][:].indirect(entries(l_n5, h)))
                if i > 0:
                    larger(i - 1)
            if h == 1:
                hand_on("out_grouped0", nc.scalar, 0, 0, HALF)
                store_words(0)
            larger(PACK - 1)
        hand_on("out_grouped1", nc.vector, 1, 0, P)
        hand_on("out_grouped2", nc.scalar, 1, P, P)
        store_words(1)
        for q in range(4):
            eng = nc.scalar if q % 2 == 0 else nc.sync
            eng.dma_start(out_2[0, 4 * q : 4 * q + 4, :].bitcast(I32), out_scales[32 * q : 32 * q + 4, :].bitcast(I32))
